import numpy as np
import ml_dtypes


def mxq(x, axis, fmt="e4m3"):
    dtype, down = {"e4m3": (ml_dtypes.float8_e4m3fn, 7), "e5m2": (ml_dtypes.float8_e5m2, 14)}[fmt]
    v = np.moveaxis(np.asarray(x, np.float32).astype(ml_dtypes.bfloat16).astype(np.float64), axis, -1)
    blocks = v.reshape(v.shape[:-1] + (-1, 32))
    amax = np.abs(blocks).max(-1, keepdims=True)
    byte = np.maximum(np.where(amax > 0, np.frexp(amax)[1] - 1 + 127, 0) - down, 1)
    scale = np.exp2(byte - 127.0)
    codes = (blocks / scale).astype(np.float32).astype(dtype).astype(np.float64)
    return np.moveaxis((codes * scale).reshape(v.shape), -1, axis)


WIDE = False


def mx_kscale(k):
    if not WIDE:
        return np.ones(k)
    levels = np.array([10, -10, 5, -5, 0])
    if k % 512:
        return np.exp2(np.random.permutation(np.resize(levels, k // 32))).repeat(32)
    a = np.empty((k // 512, 16))
    for p in range(k // 512):
        a[p, :8] = np.random.permutation(np.resize(levels, 8))
        for g in range(8):
            far = levels[np.abs(levels - a[p, g]) >= 10]
            a[p, g + 8] = far[np.random.randint(len(far))]
    return np.exp2(a.ravel()).repeat(32)


BF16 = ml_dtypes.bfloat16


def bf(x):
    return np.asarray(x, np.float32).astype(BF16)


def f64(x):
    return np.asarray(x).astype(np.float64)


E2M1 = np.array([0.0, 0.5, 1.0, 1.5, 2.0, 3.0, 4.0, 6.0, -0.0, -0.5, -1.0, -1.5, -2.0, -3.0, -4.0, -6.0])


def pack_weight(w, fmt):
    k, n = w.shape
    w = f64(bf(w)).reshape(k // 32, 32, n)
    amax = np.abs(w).max(1)
    if fmt == "e4m3":
        byte = np.frexp(amax)[1] - 1 + 127 - 7
    else:
        mant, ex = np.frexp(amax / 6.0)
        byte = np.where(mant > 0.5, ex, ex - 1) + 127
    byte = np.clip(np.where(amax > 0, byte, 1), 1, 254)
    scaled = (w * np.exp2(127.0 - byte)[:, None, :]).reshape(k, n).astype(np.float32)
    by_word = np.ascontiguousarray(scaled.reshape(k // 512, 128, 4, n).transpose(0, 1, 3, 2))
    if fmt == "e4m3":
        words = by_word.astype(ml_dtypes.float8_e4m3fn).view(np.uint8)
    else:
        c = by_word.astype(ml_dtypes.float4_e2m1fn).view(np.uint8) & 0xF
        words = c[..., 0::2] | (c[..., 1::2] << 4)
    return np.ascontiguousarray(words), np.ascontiguousarray(byte.astype(np.uint8).reshape(k // 512, 16, n))


def unpack_weight(words, scales, fmt):
    g, p, n, _ = words.shape
    if fmt == "e4m3":
        vals = np.ascontiguousarray(words).view(ml_dtypes.float8_e4m3fn).astype(np.float64)
    else:
        nib = np.empty((g, p, n, 4), np.uint8)
        nib[..., 0::2] = words & 0xF
        nib[..., 1::2] = words >> 4
        vals = E2M1[nib]
    vals = vals * np.repeat(np.exp2(scales.astype(np.float64) - 127.0), 8, axis=1)[..., None]
    return vals.transpose(0, 1, 3, 2).reshape(g * 512, n)

def planes(Y):
    n, m = Y.shape
    b = f64(bf(Y)).reshape(n // 32, 32, m)
    amax = np.abs(b).max(1)
    byte = np.clip(np.where(amax > 0, np.frexp(amax)[1] - 1 + 127 - 7, 1), 1, 254)
    codes = (b * np.exp2(127.0 - byte)[:, None, :]).reshape(n, m).astype(np.float32).astype(ml_dtypes.float8_e4m3fn).view(np.uint8)
    words = codes.reshape(n // 512, 128, 4, m).transpose(0, 1, 3, 2)
    return np.ascontiguousarray(words), np.ascontiguousarray(byte.astype(np.uint8).reshape(n // 512, 16, m))


N, D, F = 1024, 1024, 1024


def setup_inputs():
    s, t, r = mx_kscale(D), mx_kscale(F), mx_kscale(F)
    dy = bf(np.random.standard_normal((N, D)) * s)
    wd_words, wd_scales = pack_weight((np.random.standard_normal((F, D)) / np.sqrt(D) / s[None, :] * t[:, None]).T, "e4m3")
    g = bf(np.random.standard_normal((N, F)))
    u = bf(np.random.standard_normal((N, F)) * (r / t))
    wg_words, wg_scales = pack_weight((np.random.standard_normal((D, F)) / np.sqrt(F) / r[None, :]).T, "e4m3")
    wu_words, wu_scales = pack_weight((np.random.standard_normal((D, F)) / np.sqrt(F) / t[None, :]).T, "e4m3")
    return {"dy": dy,
            "wd_words": wd_words, "wd_scales": wd_scales,
            "g": g,
            "u": u,
            "wg_words": wg_words, "wg_scales": wg_scales,
            "wu_words": wu_words, "wu_scales": wu_scales}


def gate_and_up_grads(dh, g, u):
    s = 1.0 / (1.0 + np.exp(-g))
    dg = dh * u * s * (1.0 + g * (1.0 - s))
    du = dh * g * s
    return dg, du


def core(dy, wd_words, wd_scales, g, u, wg_words, wg_scales, wu_words, wu_scales):
    dh = mxq(f64(dy), 1, "e4m3") @ unpack_weight(wd_words, wd_scales, "e4m3")
    dg, du = gate_and_up_grads(dh, f64(g), f64(u))
    return (mxq(dg, 1, "e4m3") @ unpack_weight(wg_words, wg_scales, "e4m3")) + (mxq(du, 1, "e4m3") @ unpack_weight(wu_words, wu_scales, "e4m3"))


def reference(dy, wd_words, wd_scales, g, u, wg_words, wg_scales, wu_words, wu_scales):
    R_out = core(dy, wd_words, wd_scales, g, u, wg_words, wg_scales, wu_words, wu_scales)
    words, scales = planes(R_out)
    return R_out, words, scales

@@ -1,0 +1,389 @@
+from contextlib import ExitStack
+
+import concourse.mybir as mybir
+from concourse.masks import make_identity
+
+N, D, F = 1024, 1024, 1024
+FLOPS = 2 * N * D * F * 3
+
+F32 = mybir.dt.float32
+BF16 = mybir.dt.bfloat16
+I32 = mybir.dt.int32
+U32 = mybir.dt.uint32
+U8 = mybir.dt.uint8
+FP8X4 = mybir.dt.float8_e4m3fn_x4
+MULT = mybir.AluOpType.mult
+ADD = mybir.AluOpType.add
+SIGMOID = mybir.ActivationFunctionType.Sigmoid
+
+P = 128
+PACK = 4
+KP = P * PACK
+CH = 256
+NCH = N // CH
+UNITS = 2 * NCH
+
+
+def tile_swiglusavedactivationinputgradient_x2_kernel(
+    tc, dy, wd_words, wd_scales, g, u, wg_words, wg_scales, wu_words, wu_scales, out_0, out_1, out_2
+):
+    nc = tc.nc
+    with ExitStack() as ctx:
+        keep = ctx.enter_context(tc.tile_pool(name="keep", bufs=1))
+        work = ctx.enter_context(tc.tile_pool(name="work", bufs=2))
+        psum = ctx.enter_context(tc.psum_pool(name="psum", bufs=2))
+        ctx.enter_context(tc.manual_schedule())
+
+        ident = keep.tile([P, P], F32, name="ident")
+        make_identity(nc, ident[:])
+        wd_raw_s = keep.tile([P, F], U8, name="wd_raw_s", align_bytes=64)
+        nc.vector.memset(wd_raw_s[:].bitcast(I32), 0)
+        w_s = keep.tile([P, D], U8, name="w_s", align_bytes=64)
+        nc.vector.memset(w_s[:].bitcast(I32), 0)
+        wd_s = keep.tile([P, 2, PACK, P], U8, name="wd_s", align_bytes=64)
+
+        raw = {}
+        for nm in ("dy", "g", "u"):
+            for j in range(NCH):
+                if j == 0 and nm != "dy":
+                    for grp in range(2):
+                        raw[nm, j, grp] = keep.tile([P, 2, KP], BF16, name=nm + "_half" + str(grp), align_bytes=64)
+                else:
+                    raw[nm, j] = keep.tile([P, 2, D], BF16, name=nm + "_raw" + str(j), align_bytes=64)
+        wd_raw = [keep.tile([P, 2, KP], U32, name="wd_raw" + str(q), align_bytes=64) for q in range(2)]
+        wd_c = [keep.tile([P, 2, PACK, P], U32, name="wd_c" + str(q), align_bytes=64) for q in range(2)]
+        w_c = [keep.tile([P, 2, D], U32, name="w_c" + str(q), align_bytes=64) for q in range(2)]
+        res = [keep.tile([P, PACK, D], F32, name="res" + str(q), align_bytes=64) for q in range(2)]
+        res_b = [keep.tile([P, D, PACK], BF16, name="res_b" + str(q), align_bytes=64) for q in range(2)]
+        pl_c = [keep.tile([P, D], U32, name="pl_c" + str(q), align_bytes=64) for q in range(2)]
+        pl_s = [keep.tile([P, D], U8, name="pl_s" + str(q), align_bytes=64) for q in range(2)]
+
+        hbm = {"dy": dy, "g": g, "u": u}
+
+        def load(nm, j, grp=None):
+            G, c = divmod(j, 2)
+            src = hbm[nm][KP * G : KP * (G + 1), :].rearrange("(p t) d -> p t d", t=PACK)[:, 2 * c : 2 * c + 2, :]
+            if grp is None:
+                nc.sync.dma_start(out=raw[nm, j][:], in_=src)
+            else:
+                nc.sync.dma_start(out=raw[nm, j, grp][:], in_=src[:, :, KP * grp : KP * (grp + 1)])
+
+        def load_wd(gf):
+            src = wd_words[:, :, KP * gf : KP * (gf + 1), :].rearrange("k p n t -> p k (n t)").bitcast(I32)
+            nc.sync.dma_start(out=wd_raw[gf][:].bitcast(I32), in_=src)
+
+        def load_w(q):
+            src = (wg_words, wu_words)[q].rearrange("k p n t -> p k (n t)").bitcast(I32)
+            nc.sync.dma_start(out=w_c[q][:].bitcast(I32), in_=src)
+
+        def load_scales(dst, src, q0):
+            for Q in range(4):
+                r0 = 32 * Q + q0
+                nc.sync.dma_start(out=dst[r0 : r0 + 8, :].bitcast(I32), in_=src[:, 4 * Q : 4 * Q + 4, :].bitcast(I32))
+
+        load("g", 0, 0)
+        load("dy", 0)
+        load_scales(wd_raw_s, wd_scales, 0)
+        load_wd(0)
+        load("u", 0, 0)
+        load("g", 0, 1)
+        load("u", 0, 1)
+        load_wd(1)
+        load("dy", 1)
+        load("g", 1)
+        load("u", 1)
+        load("dy", 2)
+        load_w(0)
+        load_w(1)
+        load_scales(w_s, wg_scales, 0)
+        load_scales(w_s, wu_scales, 8)
+        for j in (2, 3):
+            if j == 3:
+                load("dy", 3)
+            load("g", j)
+            load("u", j)
+
+        st = {}
+
+        def turn(nm, j, grp, tag):
+            bank = psum.tile([P, 2 * CH], F32, name=tag)
+            w0 = 256 * grp
+            if (nm, j, grp) in raw:
+                words = raw[nm, j, grp][:].bitcast(F32)
+                w0 = 0
+            else:
+                words = raw[nm, j][:].bitcast(F32)
+            for v in range(2):
+                for sl in range(2):
+                    nc.tensor.transpose(
+                        bank[:, CH * v + P * sl : CH * v + P * (sl + 1)],
+                        words[:, sl, w0 + v : w0 + 256 : 2],
+                        ident[:],
+                    )
+            return bank
+
+        def TG(i):
+            st["g", i] = turn("g", i // 2, i % 2, "gt")
+
+        def TU(i):
+            st["u", i] = turn("u", i // 2, i % 2, "xt")
+
+        def TD(j, k):
+            st["d", j, k] = turn("dy", j, k, "xt")
+
+        def ED(j, k):
+            if k == 0:
+                st["dyb", j] = work.tile([P, 2, CH, PACK], BF16, name="dyb", align_bytes=64)
+            src = st["d", j, k][:].rearrange("p (v n) -> p n v", v=2)
+            dst = st["dyb", j][:, k, :, :].rearrange("p n t -> p (n t)").bitcast(F32).rearrange("p (n v) -> p n v", v=2)
+            nc.scalar.copy(dst, src)
+
+        def QD(j, k):
+            if k == 0:
+                st["dyc", j] = work.tile([P, 2, CH], U32, name="dyc", align_bytes=64)
+                st["dys", j] = work.tile([P, 2, CH], U8, name="dys", align_bytes=64)
+            nc.vector.quantize_mx(
+                out=st["dyc", j][:, k, :].bitcast(FP8X4),
+                scales=st["dys", j][:, k, :],
+                in_=st["dyb", j][:, k, :, :].rearrange("p n t -> p (n t)"),
+            )
+
+        def SG(i):
+            st["s", i] = work.tile([P, 2, CH, 2], F32, name="sg", bufs=3)
+            nc.scalar.activation(st["s", i][:].rearrange("p v n e -> p (v n e)"), st["g", i][:].bitcast(BF16), SIGMOID)
+
+        def RG(i):
+            st["r", i] = work.tile([P, 2, CH, 2], F32, name="rg", bufs=3)
+            nc.scalar.activation(
+                st["r", i][:].rearrange("p v n e -> p (v n e)"), st["g", i][:].bitcast(BF16), SIGMOID, scale=-1.0
+            )
+
+        def Z(i):
+            st["z", i] = work.tile([P, 2 * CH * 2], F32, name="zt")
+            nc.vector.tensor_tensor(
+                out=st["z", i][:], in0=st["r", i][:].rearrange("p v n e -> p (v n e)"), in1=st["g", i][:].bitcast(BF16), op=MULT
+            )
+
+        def W(i):
+            st["w", i] = work.tile([P, 2, CH, 2], F32, name="wt", bufs=3)
+            nc.vector.scalar_tensor_tensor(
+                out=st["w", i][:].rearrange("p v n e -> p (v n e)"),
+                in0=st["z", i][:],
+                scalar=1.0,
+                in1=st["u", i][:].bitcast(BF16),
+                op0=ADD,
+                op1=MULT,
+            )
+
+        def PERM_S():
+            nc.vector.tensor_copy(out=wd_s[:], in_=wd_raw_s[:].rearrange("p (f x t) -> p f t x", f=2, t=PACK))
+
+        def PERM_W(gf):
+            nc.vector.tensor_copy(
+                out=wd_c[gf][:].bitcast(I32), in_=wd_raw[gf][:].bitcast(I32).rearrange("p k (x t) -> p k t x", t=PACK)
+            )
+
+        def S1(i):
+            j, gf = divmod(i, 2)
+            for v in range(2):
+                bank = psum.tile([P, 2 * CH], F32, name="dh")
+                st["dh", i, v] = bank
+                for e in range(2):
+                    t = 2 * v + e
+                    for k in range(2):
+                        nc.tensor.matmul_mx(
+                            out=bank[:, CH * e : CH * (e + 1)],
+                            lhsT=wd_c[gf][:, k, t, :].bitcast(FP8X4),
+                            lhsT_scale=wd_s[4 * k : P, gf, t, :],
+                            rhs=st["dyc", j][:, k, :].bitcast(FP8X4),
+                            rhs_scale=st["dys", j][:, k, :],
+                            start=(k == 0),
+                            stop=(k == 1),
+                        )
+
+        def AA(i, n0=0, n1=CH):
+            if n0 == 0:
+                st["a", i] = work.tile([P, 2, CH, 2], F32, name="at", bufs=3)
+            for v in range(2):
+                nc.vector.tensor_tensor(
+                    out=st["a", i][:, v, n0:n1, :],
+                    in0=st["dh", i, v][:].rearrange("p (e n) -> p n e", e=2)[:, n0:n1, :],
+                    in1=st["s", i][:, v, n0:n1, :],
+                    op=MULT,
+                )
+
+        def gu_tile(i):
+            if ("q", i) not in st:
+                st["q", i] = work.tile([P, 2, 2, P, PACK], BF16, name="gu", align_bytes=64, bufs=3)
+                st["c", i] = work.tile([P, 2, 2, P], U32, name="guc", align_bytes=64, bufs=4)
+                st["cs", i] = work.tile([P, 2, 2, P], U8, name="gus", align_bytes=64, bufs=4)
+            return st["q", i]
+
+        def DU(i, sl):
+            ns = slice(P * sl, P * (sl + 1))
+            nc.vector.tensor_tensor(
+                out=gu_tile(i)[:, sl, 1, :, :].rearrange("p n (v e) -> p n v e", v=2),
+                in0=st["a", i][:, :, ns, :].rearrange("p v n e -> p n v e"),
+                in1=st["g", i][:].bitcast(BF16).rearrange("p (v n e) -> p n v e", v=2, e=2)[:, ns, :, :],
+                op=MULT,
+            )
+
+        def DG(i, sl, eng):
+            ns = slice(P * sl, P * (sl + 1))
+            e = nc.gpsimd if eng else nc.vector
+            e.tensor_tensor(
+                out=gu_tile(i)[:, sl, 0, :, :].rearrange("p n (v e) -> p n v e", v=2),
+                in0=st["a", i][:, :, ns, :].rearrange("p v n e -> p n v e"),
+                in1=st["w", i][:, :, ns, :].rearrange("p v n e -> p n v e"),
+                op=MULT,
+            )
+
+        def QQ(i, s0=0, s1=2):
+            nc.vector.quantize_mx(
+                out=st["c", i][:, s0:s1, :, :].rearrange("p s a n -> p (s a n)").bitcast(FP8X4),
+                scales=st["cs", i][:, s0:s1, :, :].rearrange("p s a n -> p (s a n)"),
+                in_=st["q", i][:, s0:s1, :, :, :].rearrange("p s a n t -> p (s a n t)"),
+            )
+
+        def passes(bank, j, sl, h, gfs, first, last):
+            todo = [(gf, q) for gf in gfs for q in (1, 0)]
+            for n, (gf, q) in enumerate(todo):
+                i = 2 * j + gf
+                nc.tensor.matmul_mx(
+                    out=bank[:],
+                    lhsT=st["c", i][:, sl, q, :].bitcast(FP8X4),
+                    lhsT_scale=st["cs", i][:, sl, q, :],
+                    rhs=w_c[q][:, gf, KP * h : KP * (h + 1)].bitcast(FP8X4),
+                    rhs_scale=w_s[8 * q + 4 * gf : P, KP * h : KP * (h + 1)],
+                    start=(first and n == 0),
+                    stop=(last and n == len(todo) - 1),
+                )
+
+        def EO(bank, j, sl, h, eng):
+            G, c = divmod(j, 2)
+            dst = res[G][:, 2 * c + sl, KP * h : KP * (h + 1)]
+            if eng == 0:
+                nc.scalar.copy(dst, bank[:])
+            else:
+                nc.vector.tensor_copy(out=dst, in_=bank[:])
+            rows = out_0[KP * G : KP * (G + 1), :].rearrange("(p t) d -> p t d", t=PACK)
+            nc.sync.dma_start(out=rows[:, 2 * c + sl, KP * h : KP * (h + 1)], in_=dst)
+
+        def O(G, c0, c1, eng):
+            dst = res_b[G][:, c0:c1, :]
+            src = res[G][:, :, c0:c1].rearrange("p t d -> p d t")
+            if eng == 0:
+                nc.scalar.copy(dst, src)
+            else:
+                nc.vector.tensor_copy(out=dst, in_=src)
+
+        def QO(G, h):
+            cols = slice(KP * h, KP * (h + 1))
+            nc.vector.quantize_mx(
+                out=pl_c[G][:, cols].bitcast(FP8X4),
+                scales=pl_s[G][:, cols],
+                in_=res_b[G][:, cols, :].rearrange("p d t -> p (d t)"),
+            )
+            dst = out_1[G].rearrange("p m t -> p (m t)").bitcast(I32)
+            nc.sync.dma_start(out=dst[:, cols], in_=pl_c[G][:, cols].bitcast(I32))
+            if h == 1:
+                for Q in range(4):
+                    nc.sync.dma_start(
+                        out=out_2[G, 4 * Q : 4 * Q + 4, :].bitcast(I32),
+                        in_=pl_s[G][32 * Q : 32 * Q + 4, :].bitcast(I32),
+                    )
+
+        TG(0)
+        RG(0)
+        TD(0, 0)
+        TD(0, 1)
+        ED(0, 0)
+        ED(0, 1)
+        PERM_S()
+        PERM_W(0)
+        Z(0)
+        SG(0)
+        TU(0)
+        QD(0, 0)
+        QD(0, 1)
+        S1(0)
+
+        for i in range(UNITS):
+            nxt = i + 1 < UNITS
+            jd = (i + 3) // 2
+            dk = (i + 1) % 2
+            if i > 0:
+                TU(i)
+            if nxt:
+                TG(i + 1)
+                RG(i + 1)
+                SG(i + 1)
+            if i == 0:
+                TD(1, 0)
+                ED(1, 0)
+                W(i)
+            if jd < NCH:
+                TD(jd, dk)
+                ED(jd, dk)
+            if i < 7:
+                AA(i)
+            else:
+                AA(i, 0, P)
+                AA(i, P, CH)
+            if i == 0:
+                PERM_W(1)
+                QD(1, 0)
+            if i > 0:
+                QQ(i - 1)
+                if (i + 2) // 2 < NCH:
+                    QD((i + 2) // 2, i % 2)
+                W(i)
+            if i == 7:
+                QO(0, 0)
+            if nxt:
+                S1(i + 1)
+            DG(i, 0, 1)
+            if nxt:
+                DG(i, 1, 1)
+            for sl in range(2):
+                DU(i, sl)
+            if nxt:
+                Z(i + 1)
+            if i >= 2:
+                j2 = (i - 2) // 2
+                h = i % 2
+                for sl in range(2):
+                    bank = psum.tile([P, 2 * CH], F32, name="ob")
+                    passes(bank, j2, sl, h, (0, 1), True, True)
+                    EO(bank, j2, sl, h, 0)
+            if i == 5:
+                O(0, 0, 256, 0)
+                O(0, 256, 512, 0)
+            if i == 6:
+                O(0, 512, 768, 0)
+            if i == 7:
+                O(0, 768, 1024, 0)
+        last = NCH - 1
+        banks = {}
+        for sl in range(2):
+            for h in range(2):
+                if sl == 0:
+                    bank = psum.tile([P, 2 * CH], F32, name="xt")
+                else:
+                    bank = psum.tile([P, 2 * CH], F32, name="dh")
+                banks[h, sl] = bank
+                passes(bank, last, sl, h, (0,), True, False)
+        for sl in range(2):
+            if sl == 1:
+                DG(7, 1, 0)
+            QQ(UNITS - 1, sl, sl + 1)
+            if sl == 0:
+                QO(0, 1)
+            for h in range(2):
+                passes(banks[h, sl], last, sl, h, (1,), False, True)
+                EO(banks[h, sl], last, sl, h, 0)
+        O(1, 0, 512, 1)
+        QO(1, 0)
+        O(1, 512, 768, 1)
+        O(1, 768, 1024, 0)
+        QO(1, 1)

@@ -82,8 +82,8 @@ def tile_swiglusavedactivationinputgradient_x2_kernel(
                 nc.sync.dma_start(out=dst[r0 : r0 + 8, :].bitcast(I32), in_=src[:, 4 * Q : 4 * Q + 4, :].bitcast(I32))
 
         load("g", 0, 0)
-        load("dy", 0)
         load_scales(wd_raw_s, wd_scales, 0)
+        load("dy", 0)
         load_wd(0)
         load("u", 0, 0)
         load("g", 0, 1)
@@ -269,13 +269,15 @@ def tile_swiglusavedactivationinputgradient_x2_kernel(
             rows = out_0[KP * G : KP * (G + 1), :].rearrange("(p t) d -> p t d", t=PACK)
             nc.sync.dma_start(out=rows[:, 2 * c + sl, KP * h : KP * (h + 1)], in_=dst)
 
-        def O(G, c0, c1, eng):
-            dst = res_b[G][:, c0:c1, :]
-            src = res[G][:, :, c0:c1].rearrange("p t d -> p d t")
+        def O(G, c0, c1, eng, t0=0, t1=PACK):
+            dst = res_b[G][:, c0:c1, t0:t1]
+            src = res[G][:, t0:t1, c0:c1].rearrange("p t d -> p d t")
             if eng == 0:
                 nc.scalar.copy(dst, src)
-            else:
+            elif eng == 1:
                 nc.vector.tensor_copy(out=dst, in_=src)
+            else:
+                nc.gpsimd.tensor_scalar(out=dst, in0=src, scalar1=1.0, scalar2=1.0, op0=MULT, op1=MULT)
 
         def QO(G, h):
             cols = slice(KP * h, KP * (h + 1))
@@ -300,13 +302,20 @@ def tile_swiglusavedactivationinputgradient_x2_kernel(
         ED(0, 0)
         ED(0, 1)
         PERM_S()
-        PERM_W(0)
         Z(0)
         SG(0)
         TU(0)
+        PERM_W(0)
         QD(0, 0)
         QD(0, 1)
+        W(0)
         S1(0)
+
+        def S2(i, sl):
+            j2, h = (i - 2) // 2, i % 2
+            bank = psum.tile([P, 2 * CH], F32, name="ob")
+            passes(bank, j2, sl, h, (0, 1), True, True)
+            EO(bank, j2, sl, h, 0)
 
         for i in range(UNITS):
             nxt = i + 1 < UNITS
@@ -318,29 +327,32 @@ def tile_swiglusavedactivationinputgradient_x2_kernel(
                 TG(i + 1)
                 RG(i + 1)
                 SG(i + 1)
-            if i == 0:
-                TD(1, 0)
-                ED(1, 0)
-                W(i)
-            if jd < NCH:
-                TD(jd, dk)
-                ED(jd, dk)
             if i < 7:
                 AA(i)
             else:
                 AA(i, 0, P)
                 AA(i, P, CH)
             if i == 0:
+                TD(1, 0)
+                ED(1, 0)
                 PERM_W(1)
-                QD(1, 0)
-            if i > 0:
+            else:
                 QQ(i - 1)
+                if i == 1:
+                    QD(1, 0)
                 if (i + 2) // 2 < NCH:
                     QD((i + 2) // 2, i % 2)
                 W(i)
             if i == 7:
-                QO(0, 0)
-            if nxt:
+                O(1, 0, 512, 0, 0, 2)
+            if i % 2 == 1 and i >= 2:
+                S2(i, 0)
+            if i % 2 == 0 and nxt:
+                S1(i + 1)
+            if jd < NCH:
+                TD(jd, dk)
+                ED(jd, dk)
+            if i % 2 == 1 and nxt:
                 S1(i + 1)
             DG(i, 0, 1)
             if nxt:
@@ -350,19 +362,16 @@ def tile_swiglusavedactivationinputgradient_x2_kernel(
             if nxt:
                 Z(i + 1)
             if i >= 2:
-                j2 = (i - 2) // 2
-                h = i % 2
-                for sl in range(2):
-                    bank = psum.tile([P, 2 * CH], F32, name="ob")
-                    passes(bank, j2, sl, h, (0, 1), True, True)
-                    EO(bank, j2, sl, h, 0)
+                if i % 2 == 0:
+                    S2(i, 0)
+                S2(i, 1)
             if i == 5:
                 O(0, 0, 256, 0)
-                O(0, 256, 512, 0)
             if i == 6:
-                O(0, 512, 768, 0)
+                O(0, 768, 1024, 2)
+                O(0, 256, 512, 0)
             if i == 7:
-                O(0, 768, 1024, 0)
+                O(0, 512, 768, 0)
         last = NCH - 1
         banks = {}
         for sl in range(2):
@@ -377,13 +386,13 @@ def tile_swiglusavedactivationinputgradient_x2_kernel(
             if sl == 1:
                 DG(7, 1, 0)
             QQ(UNITS - 1, sl, sl + 1)
-            if sl == 0:
-                QO(0, 1)
             for h in range(2):
                 passes(banks[h, sl], last, sl, h, (1,), False, True)
                 EO(banks[h, sl], last, sl, h, 0)
-        O(1, 0, 512, 1)
+        O(1, 512, 1024, 1, 0, 2)
+        QO(0, 0)
+        QO(0, 1)
+        O(1, 0, 512, 1, 2, 4)
         QO(1, 0)
-        O(1, 512, 768, 1)
-        O(1, 768, 1024, 0)
+        O(1, 512, 1024, 1, 2, 4)
         QO(1, 1)

@@ -207,43 +207,61 @@ def tile_swiglusavedactivationinputgradient_x2_kernel(
             for v in range(2):
                 nc.vector.tensor_tensor(
                     out=st["a", i][:, v, n0:n1, :],
-                    in0=st["dh", i, v][:].rearrange("p (e n) -> p n e", e=2)[:, n0:n1, :],
-                    in1=st["s", i][:, v, n0:n1, :],
+                    in0=st["s", i][:, v, n0:n1, :],
+                    in1=st["dh", i, v][:].rearrange("p (e n) -> p n e", e=2)[:, n0:n1, :],
                     op=MULT,
                 )
 
+        def parts(i):
+            return (CH,) if i < UNITS - 1 else (P, P)
+
         def gu_tile(i):
             if ("q", i) not in st:
-                st["q", i] = work.tile([P, 2, 2, P, PACK], BF16, name="gu", align_bytes=64, bufs=3)
-                st["c", i] = work.tile([P, 2, 2, P], U32, name="guc", align_bytes=64, bufs=4)
-                st["cs", i] = work.tile([P, 2, 2, P], U8, name="gus", align_bytes=64, bufs=4)
+                st["q", i] = work.tile([P, 2 * CH * PACK], BF16, name="gu", align_bytes=64, bufs=3)
+                st["c", i] = work.tile([P, 2 * CH], U32, name="guc", align_bytes=64, bufs=4)
+                st["cs", i] = work.tile([P, 2 * CH], U8, name="gus", align_bytes=64, bufs=4)
             return st["q", i]
 
-        def DU(i, sl):
-            ns = slice(P * sl, P * (sl + 1))
+        def gu_out(i, part, kind):
+            w = parts(i)[0]
+            off = (2 * part + kind) * w * PACK
+            return gu_tile(i)[:, off : off + w * PACK].rearrange("p (n v e) -> p n v e", v=2, e=2)
+
+        def rows_of(i, part):
+            w = parts(i)[0]
+            return slice(w * part, w * (part + 1))
+
+        def DU(i, part):
+            ns = rows_of(i, part)
             nc.vector.tensor_tensor(
-                out=gu_tile(i)[:, sl, 1, :, :].rearrange("p n (v e) -> p n v e", v=2),
+                out=gu_out(i, part, 1),
                 in0=st["a", i][:, :, ns, :].rearrange("p v n e -> p n v e"),
                 in1=st["g", i][:].bitcast(BF16).rearrange("p (v n e) -> p n v e", v=2, e=2)[:, ns, :, :],
                 op=MULT,
             )
 
-        def DG(i, sl, eng):
-            ns = slice(P * sl, P * (sl + 1))
+        def DG(i, part, eng):
+            ns = rows_of(i, part)
             e = nc.gpsimd if eng else nc.vector
             e.tensor_tensor(
-                out=gu_tile(i)[:, sl, 0, :, :].rearrange("p n (v e) -> p n v e", v=2),
+                out=gu_out(i, part, 0),
                 in0=st["a", i][:, :, ns, :].rearrange("p v n e -> p n v e"),
                 in1=st["w", i][:, :, ns, :].rearrange("p v n e -> p n v e"),
                 op=MULT,
             )
 
-        def QQ(i, s0=0, s1=2):
+        def QQ(i, part=0):
+            w = parts(i)[0]
+            cols = slice(2 * w * part, 2 * w * (part + 1))
             nc.vector.quantize_mx(
-                out=st["c", i][:, s0:s1, :, :].rearrange("p s a n -> p (s a n)").bitcast(FP8X4),
-                scales=st["cs", i][:, s0:s1, :, :].rearrange("p s a n -> p (s a n)"),
-                in_=st["q", i][:, s0:s1, :, :, :].rearrange("p s a n t -> p (s a n t)"),
+                out=st["c", i][:, cols].bitcast(FP8X4),
+                scales=st["cs", i][:, cols],
+                in_=st["q", i][:, 2 * w * PACK * part : 2 * w * PACK * (part + 1)],
             )
+
+        def code_cols(i, sl, q):
+            c0 = CH * q + P * sl if len(parts(i)) == 1 else CH * sl + P * q
+            return slice(c0, c0 + P)
 
         def passes(bank, j, sl, h, gfs, first, last):
             todo = [(gf, q) for gf in gfs for q in (1, 0)]
@@ -251,8 +269,8 @@ def tile_swiglusavedactivationinputgradient_x2_kernel(
                 i = 2 * j + gf
                 nc.tensor.matmul_mx(
                     out=bank[:],
-                    lhsT=st["c", i][:, sl, q, :].bitcast(FP8X4),
-                    lhsT_scale=st["cs", i][:, sl, q, :],
+                    lhsT=st["c", i][:, code_cols(i, sl, q)].bitcast(FP8X4),
+                    lhsT_scale=st["cs", i][:, code_cols(i, sl, q)],
                     rhs=w_c[q][:, gf, KP * h : KP * (h + 1)].bitcast(FP8X4),
                     rhs_scale=w_s[8 * q + 4 * gf : P, KP * h : KP * (h + 1)],
                     start=(first and n == 0),
@@ -267,7 +285,10 @@ def tile_swiglusavedactivationinputgradient_x2_kernel(
             else:
                 nc.vector.tensor_copy(out=dst, in_=bank[:])
             rows = out_0[KP * G : KP * (G + 1), :].rearrange("(p t) d -> p t d", t=PACK)
-            nc.sync.dma_start(out=rows[:, 2 * c + sl, KP * h : KP * (h + 1)], in_=dst)
+            if j < NCH - 1:
+                nc.sync.dma_start(out=rows[:, 2 * c + sl, KP * h : KP * (h + 1)], in_=dst)
+            elif h == 1:
+                nc.sync.dma_start(out=rows[:, 2 * c + sl, :], in_=res[G][:, 2 * c + sl, :])
 
         def O(G, c0, c1, eng, t0=0, t1=PACK):
             dst = res_b[G][:, c0:c1, t0:t1]
@@ -330,19 +351,22 @@ def tile_swiglusavedactivationinputgradient_x2_kernel(
             if i < 7:
                 AA(i)
             else:
+                QQ(i - 1)
+                W(i)
                 AA(i, 0, P)
+                DG(i, 0, 1)
                 AA(i, P, CH)
             if i == 0:
                 TD(1, 0)
                 ED(1, 0)
                 PERM_W(1)
-            else:
-                QQ(i - 1)
+            elif i < 7:
                 if i == 1:
                     QD(1, 0)
                 if (i + 2) // 2 < NCH:
                     QD((i + 2) // 2, i % 2)
                 W(i)
+                QQ(i - 1)
             if i == 7:
                 O(1, 0, 512, 0, 0, 2)
             if i % 2 == 1 and i >= 2:
@@ -354,11 +378,10 @@ def tile_swiglusavedactivationinputgradient_x2_kernel(
                 ED(jd, dk)
             if i % 2 == 1 and nxt:
                 S1(i + 1)
-            DG(i, 0, 1)
-            if nxt:
-                DG(i, 1, 1)
-            for sl in range(2):
-                DU(i, sl)
+            if i < 7:
+                DG(i, 0, 1)
+            for part in range(len(parts(i))):
+                DU(i, part)
             if nxt:
                 Z(i + 1)
             if i >= 2:
@@ -368,7 +391,6 @@ def tile_swiglusavedactivationinputgradient_x2_kernel(
             if i == 5:
                 O(0, 0, 256, 0)
             if i == 6:
-                O(0, 768, 1024, 2)
                 O(0, 256, 512, 0)
             if i == 7:
                 O(0, 512, 768, 0)
@@ -385,14 +407,16 @@ def tile_swiglusavedactivationinputgradient_x2_kernel(
         for sl in range(2):
             if sl == 1:
                 DG(7, 1, 0)
-            QQ(UNITS - 1, sl, sl + 1)
+            QQ(UNITS - 1, sl)
+            if sl == 1:
+                O(0, 768, 1024, 1)
+                QO(0, 0)
+                QO(0, 1)
             for h in range(2):
                 passes(banks[h, sl], last, sl, h, (1,), False, True)
                 EO(banks[h, sl], last, sl, h, 0)
         O(1, 512, 1024, 1, 0, 2)
-        QO(0, 0)
-        QO(0, 1)
         O(1, 0, 512, 1, 2, 4)
+        O(1, 512, 1024, 0, 2, 4)
         QO(1, 0)
-        O(1, 512, 1024, 1, 2, 4)
         QO(1, 1)

from contextlib import ExitStack

import concourse.mybir as mybir
from concourse.masks import make_identity

N, D, F = 1024, 1024, 1024
FLOPS = 2 * N * D * F * 3

F32 = mybir.dt.float32
BF16 = mybir.dt.bfloat16
I32 = mybir.dt.int32
U32 = mybir.dt.uint32
U8 = mybir.dt.uint8
FP8X4 = mybir.dt.float8_e4m3fn_x4
MULT = mybir.AluOpType.mult
ADD = mybir.AluOpType.add
SIGMOID = mybir.ActivationFunctionType.Sigmoid

P = 128
PACK = 4
KP = P * PACK
CH = 256
NCH = N // CH
UNITS = 2 * NCH


def tile_swiglusavedactivationinputgradient_x2_kernel(
    tc, dy, wd_words, wd_scales, g, u, wg_words, wg_scales, wu_words, wu_scales, out_0, out_1, out_2
):
    nc = tc.nc
    with ExitStack() as ctx:
        keep = ctx.enter_context(tc.tile_pool(name="keep", bufs=1))
        work = ctx.enter_context(tc.tile_pool(name="work", bufs=2))
        psum = ctx.enter_context(tc.psum_pool(name="psum", bufs=2))
        ctx.enter_context(tc.manual_schedule())

        ident = keep.tile([P, P], F32, name="ident")
        make_identity(nc, ident[:])
        wd_raw_s = keep.tile([P, F], U8, name="wd_raw_s", align_bytes=64)
        nc.vector.memset(wd_raw_s[:].bitcast(I32), 0)
        w_s = keep.tile([P, D], U8, name="w_s", align_bytes=64)
        nc.vector.memset(w_s[:].bitcast(I32), 0)
        wd_s = keep.tile([P, 2, PACK, P], U8, name="wd_s", align_bytes=64)

        raw = {}
        for nm in ("dy", "g", "u"):
            for j in range(NCH):
                if j == 0 and nm != "dy":
                    for grp in range(2):
                        raw[nm, j, grp] = keep.tile([P, 2, KP], BF16, name=nm + "_half" + str(grp), align_bytes=64)
                else:
                    raw[nm, j] = keep.tile([P, 2, D], BF16, name=nm + "_raw" + str(j), align_bytes=64)
        wd_raw = [keep.tile([P, 2, KP], U32, name="wd_raw" + str(q), align_bytes=64) for q in range(2)]
        wd_c = [keep.tile([P, 2, PACK, P], U32, name="wd_c" + str(q), align_bytes=64) for q in range(2)]
        w_c = [keep.tile([P, 2, D], U32, name="w_c" + str(q), align_bytes=64) for q in range(2)]
        res = [keep.tile([P, PACK, D], F32, name="res" + str(q), align_bytes=64) for q in range(2)]
        res_b = [keep.tile([P, D, PACK], BF16, name="res_b" + str(q), align_bytes=64) for q in range(2)]
        pl_c = [keep.tile([P, D], U32, name="pl_c" + str(q), align_bytes=64) for q in range(2)]
        pl_s = [keep.tile([P, D], U8, name="pl_s" + str(q), align_bytes=64) for q in range(2)]

        hbm = {"dy": dy, "g": g, "u": u}

        def load(nm, j, grp=None):
            G, c = divmod(j, 2)
            src = hbm[nm][KP * G : KP * (G + 1), :].rearrange("(p t) d -> p t d", t=PACK)[:, 2 * c : 2 * c + 2, :]
            if grp is None:
                nc.sync.dma_start(out=raw[nm, j][:], in_=src)
            else:
                nc.sync.dma_start(out=raw[nm, j, grp][:], in_=src[:, :, KP * grp : KP * (grp + 1)])

        def load_wd(gf):
            src = wd_words[:, :, KP * gf : KP * (gf + 1), :].rearrange("k p n t -> p k (n t)").bitcast(I32)
            nc.sync.dma_start(out=wd_raw[gf][:].bitcast(I32), in_=src)

        def load_w(q):
            src = (wg_words, wu_words)[q].rearrange("k p n t -> p k (n t)").bitcast(I32)
            nc.sync.dma_start(out=w_c[q][:].bitcast(I32), in_=src)

        def load_scales(dst, src, q0):
            for Q in range(4):
                r0 = 32 * Q + q0
                nc.sync.dma_start(out=dst[r0 : r0 + 8, :].bitcast(I32), in_=src[:, 4 * Q : 4 * Q + 4, :].bitcast(I32))

        load("g", 0, 0)
        load_scales(wd_raw_s, wd_scales, 0)
        load("dy", 0)
        load_wd(0)
        load("u", 0, 0)
        load("g", 0, 1)
        load("u", 0, 1)
        load_wd(1)
        load("dy", 1)
        load("g", 1)
        load("u", 1)
        load("dy", 2)
        load_w(0)
        load_w(1)
        load_scales(w_s, wg_scales, 0)
        load_scales(w_s, wu_scales, 8)
        for j in (2, 3):
            if j == 3:
                load("dy", 3)
            load("g", j)
            load("u", j)

        st = {}

        def turn(nm, j, grp, tag):
            bank = psum.tile([P, 2 * CH], F32, name=tag)
            w0 = 256 * grp
            if (nm, j, grp) in raw:
                words = raw[nm, j, grp][:].bitcast(F32)
                w0 = 0
            else:
                words = raw[nm, j][:].bitcast(F32)
            for v in range(2):
                for sl in range(2):
                    nc.tensor.transpose(
                        bank[:, CH * v + P * sl : CH * v + P * (sl + 1)],
                        words[:, sl, w0 + v : w0 + 256 : 2],
                        ident[:],
                    )
            return bank

        def TG(i):
            st["g", i] = turn("g", i // 2, i % 2, "gt")

        def TU(i):
            st["u", i] = turn("u", i // 2, i % 2, "xt")

        def TD(j, k):
            st["d", j, k] = turn("dy", j, k, "xt")

        def ED(j, k):
            if k == 0:
                st["dyb", j] = work.tile([P, 2, CH, PACK], BF16, name="dyb", align_bytes=64)
            src = st["d", j, k][:].rearrange("p (v n) -> p n v", v=2)
            dst = st["dyb", j][:, k, :, :].rearrange("p n t -> p (n t)").bitcast(F32).rearrange("p (n v) -> p n v", v=2)
            nc.scalar.copy(dst, src)

        def QD(j, k):
            if k == 0:
                st["dyc", j] = work.tile([P, 2, CH], U32, name="dyc", align_bytes=64)
                st["dys", j] = work.tile([P, 2, CH], U8, name="dys", align_bytes=64)
            nc.vector.quantize_mx(
                out=st["dyc", j][:, k, :].bitcast(FP8X4),
                scales=st["dys", j][:, k, :],
                in_=st["dyb", j][:, k, :, :].rearrange("p n t -> p (n t)"),
            )

        def SG(i):
            st["s", i] = work.tile([P, 2, CH, 2], F32, name="sg", bufs=3)
            nc.scalar.activation(st["s", i][:].rearrange("p v n e -> p (v n e)"), st["g", i][:].bitcast(BF16), SIGMOID)

        def RG(i):
            st["r", i] = work.tile([P, 2, CH, 2], F32, name="rg", bufs=3)
            nc.scalar.activation(
                st["r", i][:].rearrange("p v n e -> p (v n e)"), st["g", i][:].bitcast(BF16), SIGMOID, scale=-1.0
            )

        def Z(i):
            st["z", i] = work.tile([P, 2 * CH * 2], F32, name="zt")
            nc.vector.tensor_tensor(
                out=st["z", i][:], in0=st["r", i][:].rearrange("p v n e -> p (v n e)"), in1=st["g", i][:].bitcast(BF16), op=MULT
            )

        def W(i):
            st["w", i] = work.tile([P, 2, CH, 2], F32, name="wt", bufs=3)
            nc.vector.scalar_tensor_tensor(
                out=st["w", i][:].rearrange("p v n e -> p (v n e)"),
                in0=st["z", i][:],
                scalar=1.0,
                in1=st["u", i][:].bitcast(BF16),
                op0=ADD,
                op1=MULT,
            )

        def PERM_S():
            nc.vector.tensor_copy(out=wd_s[:], in_=wd_raw_s[:].rearrange("p (f x t) -> p f t x", f=2, t=PACK))

        def PERM_W(gf):
            nc.vector.tensor_copy(
                out=wd_c[gf][:].bitcast(I32), in_=wd_raw[gf][:].bitcast(I32).rearrange("p k (x t) -> p k t x", t=PACK)
            )

        def S1(i):
            j, gf = divmod(i, 2)
            for v in range(2):
                bank = psum.tile([P, 2 * CH], F32, name="dh")
                st["dh", i, v] = bank
                for e in range(2):
                    t = 2 * v + e
                    for k in range(2):
                        nc.tensor.matmul_mx(
                            out=bank[:, CH * e : CH * (e + 1)],
                            lhsT=wd_c[gf][:, k, t, :].bitcast(FP8X4),
                            lhsT_scale=wd_s[4 * k : P, gf, t, :],
                            rhs=st["dyc", j][:, k, :].bitcast(FP8X4),
                            rhs_scale=st["dys", j][:, k, :],
                            start=(k == 0),
                            stop=(k == 1),
                        )

        def AA(i, n0=0, n1=CH):
            if n0 == 0:
                st["a", i] = work.tile([P, 2, CH, 2], F32, name="at", bufs=3)
            for v in range(2):
                nc.vector.tensor_tensor(
                    out=st["a", i][:, v, n0:n1, :],
                    in0=st["s", i][:, v, n0:n1, :],
                    in1=st["dh", i, v][:].rearrange("p (e n) -> p n e", e=2)[:, n0:n1, :],
                    op=MULT,
                )

        def parts(i):
            return (CH,) if i < UNITS - 1 else (P, P)

        def gu_tile(i):
            if ("q", i) not in st:
                st["q", i] = work.tile([P, 2 * CH * PACK], BF16, name="gu", align_bytes=64, bufs=3)
                st["c", i] = work.tile([P, 2 * CH], U32, name="guc", align_bytes=64, bufs=4)
                st["cs", i] = work.tile([P, 2 * CH], U8, name="gus", align_bytes=64, bufs=4)
            return st["q", i]

        def gu_out(i, part, kind):
            w = parts(i)[0]
            off = (2 * part + kind) * w * PACK
            return gu_tile(i)[:, off : off + w * PACK].rearrange("p (n v e) -> p n v e", v=2, e=2)

        def rows_of(i, part):
            w = parts(i)[0]
            return slice(w * part, w * (part + 1))

        def DU(i, part):
            ns = rows_of(i, part)
            nc.vector.tensor_tensor(
                out=gu_out(i, part, 1),
                in0=st["a", i][:, :, ns, :].rearrange("p v n e -> p n v e"),
                in1=st["g", i][:].bitcast(BF16).rearrange("p (v n e) -> p n v e", v=2, e=2)[:, ns, :, :],
                op=MULT,
            )

        def DG(i, part, eng):
            ns = rows_of(i, part)
            e = nc.gpsimd if eng else nc.vector
            e.tensor_tensor(
                out=gu_out(i, part, 0),
                in0=st["a", i][:, :, ns, :].rearrange("p v n e -> p n v e"),
                in1=st["w", i][:, :, ns, :].rearrange("p v n e -> p n v e"),
                op=MULT,
            )

        def QQ(i, part=0):
            w = parts(i)[0]
            cols = slice(2 * w * part, 2 * w * (part + 1))
            nc.vector.quantize_mx(
                out=st["c", i][:, cols].bitcast(FP8X4),
                scales=st["cs", i][:, cols],
                in_=st["q", i][:, 2 * w * PACK * part : 2 * w * PACK * (part + 1)],
            )

        def code_cols(i, sl, q):
            c0 = CH * q + P * sl if len(parts(i)) == 1 else CH * sl + P * q
            return slice(c0, c0 + P)

        def passes(bank, j, sl, h, gfs, first, last):
            todo = [(gf, q) for gf in gfs for q in (1, 0)]
            for n, (gf, q) in enumerate(todo):
                i = 2 * j + gf
                nc.tensor.matmul_mx(
                    out=bank[:],
                    lhsT=st["c", i][:, code_cols(i, sl, q)].bitcast(FP8X4),
                    lhsT_scale=st["cs", i][:, code_cols(i, sl, q)],
                    rhs=w_c[q][:, gf, KP * h : KP * (h + 1)].bitcast(FP8X4),
                    rhs_scale=w_s[8 * q + 4 * gf : P, KP * h : KP * (h + 1)],
                    start=(first and n == 0),
                    stop=(last and n == len(todo) - 1),
                )

        def EO(bank, j, sl, h, eng):
            G, c = divmod(j, 2)
            dst = res[G][:, 2 * c + sl, KP * h : KP * (h + 1)]
            if eng == 0:
                nc.scalar.copy(dst, bank[:])
            else:
                nc.vector.tensor_copy(out=dst, in_=bank[:])
            rows = out_0[KP * G : KP * (G + 1), :].rearrange("(p t) d -> p t d", t=PACK)
            if j < NCH - 1:
                nc.sync.dma_start(out=rows[:, 2 * c + sl, KP * h : KP * (h + 1)], in_=dst)
            elif h == 1:
                nc.sync.dma_start(out=rows[:, 2 * c + sl, :], in_=res[G][:, 2 * c + sl, :])

        def O(G, c0, c1, eng, t0=0, t1=PACK):
            dst = res_b[G][:, c0:c1, t0:t1]
            src = res[G][:, t0:t1, c0:c1].rearrange("p t d -> p d t")
            if eng == 0:
                nc.scalar.copy(dst, src)
            elif eng == 1:
                nc.vector.tensor_copy(out=dst, in_=src)
            else:
                nc.gpsimd.tensor_scalar(out=dst, in0=src, scalar1=1.0, scalar2=1.0, op0=MULT, op1=MULT)

        def QO(G, h):
            cols = slice(KP * h, KP * (h + 1))
            nc.vector.quantize_mx(
                out=pl_c[G][:, cols].bitcast(FP8X4),
                scales=pl_s[G][:, cols],
                in_=res_b[G][:, cols, :].rearrange("p d t -> p (d t)"),
            )
            dst = out_1[G].rearrange("p m t -> p (m t)").bitcast(I32)
            nc.sync.dma_start(out=dst[:, cols], in_=pl_c[G][:, cols].bitcast(I32))
            if h == 1:
                for Q in range(4):
                    nc.sync.dma_start(
                        out=out_2[G, 4 * Q : 4 * Q + 4, :].bitcast(I32),
                        in_=pl_s[G][32 * Q : 32 * Q + 4, :].bitcast(I32),
                    )

        TG(0)
        RG(0)
        TD(0, 0)
        TD(0, 1)
        ED(0, 0)
        ED(0, 1)
        PERM_S()
        Z(0)
        SG(0)
        TU(0)
        PERM_W(0)
        QD(0, 0)
        QD(0, 1)
        W(0)
        S1(0)

        def S2(i, sl):
            j2, h = (i - 2) // 2, i % 2
            bank = psum.tile([P, 2 * CH], F32, name="ob")
            passes(bank, j2, sl, h, (0, 1), True, True)
            EO(bank, j2, sl, h, 0)

        for i in range(UNITS):
            nxt = i + 1 < UNITS
            jd = (i + 3) // 2
            dk = (i + 1) % 2
            if i > 0:
                TU(i)
            if nxt:
                TG(i + 1)
                RG(i + 1)
                SG(i + 1)
            if i < 7:
                AA(i)
            else:
                QQ(i - 1)
                W(i)
                AA(i, 0, P)
                DG(i, 0, 1)
                AA(i, P, CH)
            if i == 0:
                TD(1, 0)
                ED(1, 0)
                PERM_W(1)
            elif i < 7:
                if i == 1:
                    QD(1, 0)
                if (i + 2) // 2 < NCH:
                    QD((i + 2) // 2, i % 2)
                W(i)
                QQ(i - 1)
            if i == 7:
                O(1, 0, 512, 0, 0, 2)
            if i % 2 == 1 and i >= 2:
                S2(i, 0)
            if i % 2 == 0 and nxt:
                S1(i + 1)
            if jd < NCH:
                TD(jd, dk)
                ED(jd, dk)
            if i % 2 == 1 and nxt:
                S1(i + 1)
            if i < 7:
                DG(i, 0, 1)
            for part in range(len(parts(i))):
                DU(i, part)
            if nxt:
                Z(i + 1)
            if i >= 2:
                if i % 2 == 0:
                    S2(i, 0)
                S2(i, 1)
            if i == 5:
                O(0, 0, 256, 0)
            if i == 6:
                O(0, 256, 512, 0)
            if i == 7:
                O(0, 512, 768, 0)
        last = NCH - 1
        banks = {}
        for sl in range(2):
            for h in range(2):
                if sl == 0:
                    bank = psum.tile([P, 2 * CH], F32, name="xt")
                else:
                    bank = psum.tile([P, 2 * CH], F32, name="dh")
                banks[h, sl] = bank
                passes(bank, last, sl, h, (0,), True, False)
        for sl in range(2):
            if sl == 1:
                DG(7, 1, 0)
            QQ(UNITS - 1, sl)
            if sl == 1:
                O(0, 768, 1024, 1)
                QO(0, 0)
                QO(0, 1)
            for h in range(2):
                passes(banks[h, sl], last, sl, h, (1,), False, True)
                EO(banks[h, sl], last, sl, h, 0)
        O(1, 512, 1024, 1, 0, 2)
        O(1, 0, 512, 1, 2, 4)
        O(1, 512, 1024, 0, 2, 4)
        QO(1, 0)
        QO(1, 1)
